import numpy as np
import ml_dtypes


def mxq(x, axis, fmt="e4m3"):
    dtype, down = {"e4m3": (ml_dtypes.float8_e4m3fn, 7), "e5m2": (ml_dtypes.float8_e5m2, 14)}[fmt]
    v = np.moveaxis(np.asarray(x, np.float32).astype(ml_dtypes.bfloat16).astype(np.float64), axis, -1)
    blocks = v.reshape(v.shape[:-1] + (-1, 32))
    amax = np.abs(blocks).max(-1, keepdims=True)
    byte = np.maximum(np.where(amax > 0, np.frexp(amax)[1] - 1 + 127, 0) - down, 1)
    scale = np.exp2(byte - 127.0)
    codes = (blocks / scale).astype(np.float32).astype(dtype).astype(np.float64)
    return np.moveaxis((codes * scale).reshape(v.shape), -1, axis)


WIDE = False


def mx_kscale(k):
    if not WIDE:
        return np.ones(k)
    levels = np.array([10, -10, 5, -5, 0])
    if k % 512:
        return np.exp2(np.random.permutation(np.resize(levels, k // 32))).repeat(32)
    a = np.empty((k // 512, 16))
    for p in range(k // 512):
        a[p, :8] = np.random.permutation(np.resize(levels, 8))
        for g in range(8):
            far = levels[np.abs(levels - a[p, g]) >= 10]
            a[p, g + 8] = far[np.random.randint(len(far))]
    return np.exp2(a.ravel()).repeat(32)


def f64(x):
    return np.asarray(x).astype(np.float64)


def striped(idx):
    return np.tile(idx.reshape(-1, 16).T, (8, 1)).astype(np.uint16)


def unstriped(offs):
    return offs[:16].T.reshape(-1).astype(np.int64)


E2M1 = np.array([0.0, 0.5, 1.0, 1.5, 2.0, 3.0, 4.0, 6.0, -0.0, -0.5, -1.0, -1.5, -2.0, -3.0, -4.0, -6.0])


def pack_weight(w, fmt):
    k, n = w.shape
    w = f64(np.asarray(w, np.float32).astype(ml_dtypes.bfloat16)).reshape(k // 32, 32, n)
    amax = np.abs(w).max(1)
    if fmt == "e4m3":
        byte = np.frexp(amax)[1] - 1 + 127 - 7
    else:
        mant, ex = np.frexp(amax / 6.0)
        byte = np.where(mant > 0.5, ex, ex - 1) + 127
    byte = np.clip(np.where(amax > 0, byte, 1), 1, 254)
    scaled = (w * np.exp2(127.0 - byte)[:, None, :]).reshape(k, n).astype(np.float32)
    by_word = np.ascontiguousarray(scaled.reshape(k // 512, 128, 4, n).transpose(0, 1, 3, 2))
    if fmt == "e4m3":
        words = by_word.astype(ml_dtypes.float8_e4m3fn).view(np.uint8)
    else:
        c = by_word.astype(ml_dtypes.float4_e2m1fn).view(np.uint8) & 0xF
        words = (c[..., 0::2] | (c[..., 1::2] << 4)).reshape(k // 512, 128, 2 * n)
    return np.ascontiguousarray(words), np.ascontiguousarray(byte.astype(np.uint8).reshape(k // 512, 16, n))


def unpack_weight(words, scales, fmt):
    g, _, n = scales.shape
    words = np.ascontiguousarray(words).reshape(g, 128, n, -1)
    if fmt == "e4m3":
        vals = words.view(ml_dtypes.float8_e4m3fn).astype(np.float64)
    else:
        nib = np.empty((g, 128, n, 4), np.uint8)
        nib[..., 0::2] = words & 0xF
        nib[..., 1::2] = words >> 4
        vals = E2M1[nib]
    vals = vals * np.repeat(np.exp2(scales.astype(np.float64) - 127.0), 8, axis=1)[..., None]
    return vals.transpose(0, 1, 3, 2).reshape(g * 512, n)


def relu(v):
    return np.maximum(v, 0.0)


K, T, E, C, H, N = 1536, 512, 4, 128, 512, 256
R = 4


def by_expert(wq, xq):
    return np.concatenate([wq[e].T @ xq[:, e * C:(e + 1) * C] for e in range(E)], axis=1)


def setup_inputs():
    n = np.random.standard_normal
    s = mx_kscale(K)[:, None]
    u = mx_kscale(H)
    slot_token = np.concatenate([r * (T // R) + np.random.permutation(T // R)[:C // R] for e in range(E) for r in range(R)])
    w1 = [pack_weight(m, "e2m1") for m in n((E, K, H)) / np.sqrt(K) / s[None]]
    w3 = [pack_weight(m, "e2m1") for m in n((E, K, H)) / np.sqrt(K) / s[None] * u[None, None, :]]
    w2 = [pack_weight(m, "e2m1") for m in n((E, H, N)) / np.sqrt(H) / u[None, :, None]]
    return {
        "xT": (n((K, T)) * s).astype(np.float32),
        "w1_words": np.stack([m[0] for m in w1]),
        "w1_scales": np.stack([m[1] for m in w1]),
        "w3_words": np.stack([m[0] for m in w3]),
        "w3_scales": np.stack([m[1] for m in w3]),
        "w2_words": np.stack([m[0] for m in w2]),
        "w2_scales": np.stack([m[1] for m in w2]),
        "offs": striped(slot_token),
    }


def reference(xT, w1_words, w1_scales, w3_words, w3_scales, w2_words, w2_scales, offs):
    idx = unstriped(offs)
    w1 = np.stack([unpack_weight(w1_words[e], w1_scales[e], "e2m1") for e in range(E)])
    w3 = np.stack([unpack_weight(w3_words[e], w3_scales[e], "e2m1") for e in range(E)])
    w2 = np.stack([unpack_weight(w2_words[e], w2_scales[e], "e2m1") for e in range(E)])
    xq = mxq(f64(xT)[:, idx], 0, "e4m3")
    h = relu(by_expert(w1, xq))
    h = h * by_expert(w3, xq)
    y = by_expert(w2, mxq(h, 0, "e4m3"))
    return y.reshape(N, E, R, C // R).transpose(0, 2, 1, 3).reshape(N, E * C)

from contextlib import ExitStack

import concourse.mybir as mybir
from concourse.masks import make_identity

K, T, E, C, H, N = 1536, 512, 4, 128, 512, 256
R = 4
P = 128
PASSES = K // 512
FLOPS = E * (2 * 2 * K * C * H + 2 * H * C * N)

F32 = mybir.dt.float32
BF16 = mybir.dt.bfloat16
U32 = mybir.dt.uint32
I32 = mybir.dt.int32
U16 = mybir.dt.uint16
U8 = mybir.dt.uint8
E4M3 = mybir.dt.float8_e4m3fn_x4
E2M1 = mybir.dt.float4_e2m1fn_x4
COPY = mybir.ActivationFunctionType.Copy
RELU = mybir.ActivationFunctionType.Relu
MULT = mybir.AluOpType.mult

CHUNKS = ((0, 0, 160, 256), (0, 256, 416, 512), (1, 0, 64, 512), (2, 0, 128, 512))


def tile_moe_eps_glu_relu_kernel(
    tc, xT, w1_words, w1_scales, w3_words, w3_scales, w2_words, w2_scales, offs, out
):
    nc = tc.nc
    with ExitStack() as ctx:
        keep = ctx.enter_context(tc.tile_pool(name="keep", bufs=1))
        work = ctx.enter_context(tc.tile_pool(name="work", bufs=3))
        psum = ctx.enter_context(tc.psum_pool(name="psum", bufs=3))
        psum1 = ctx.enter_context(tc.psum_pool(name="psum1", bufs=1))

        offsets = keep.tile([P, E * C // 16], U16, name="offsets")
        x_raw = [keep.tile([P, 4, T], F32, name=f"x_raw{s}") for s in range(PASSES)]
        x_grp = [keep.tile([P, T, 4], BF16, name=f"x_grp{s}", align_bytes=64) for s in range(PASSES)]
        x_words = [keep.tile([P, T], U32, name=f"x_words{s}", align_bytes=64) for s in range(PASSES)]
        x_bytes = [keep.tile([P, T], U8, name=f"x_bytes{s}", align_bytes=64) for s in range(PASSES)]
        g_words = [keep.tile([P, E * C], U32, name=f"g_words{s}", align_bytes=64) for s in range(PASSES)]
        g_bytes = [keep.tile([P, E * C], U8, name=f"g_bytes{s}", align_bytes=64) for s in range(PASSES)]
        w13 = keep.tile([P, E, 2, PASSES, 2 * H], U8, name="w13", align_bytes=64)
        w2_t = keep.tile([P, E, 2 * N], U8, name="w2_t", align_bytes=64)
        sc13 = [keep.tile([P, 2, 2 * PASSES, H], U8, name=f"sc13_{f}", align_bytes=64) for f in range(2)]
        sc2 = keep.tile([P, E, N], U8, name="sc2", align_bytes=64)
        ident = keep.tile([P, P], F32, name="ident")
        o_sb = keep.tile([P, 2, R, E, C // R], F32, name="o_sb")

        nc.vector.memset(sc13[0][:].bitcast(I32), 0)
        for s in range(PASSES):
            nc.gpsimd.memset(x_bytes[s][:], 0)
        nc.vector.memset(sc13[1][:].bitcast(I32), 0)
        nc.vector.memset(sc2[:].bitcast(I32), 0)
        nc.vector.memset(x_raw[2][:, :, 0:2], 0.0)
        nc.vector.memset(w13[:].rearrange("p e m s c -> p (e m s) c").bitcast(I32)[:, :, 0:1], 0)
        nc.vector.memset(w2_t[:].bitcast(I32)[:, :, 0:1], 0)
        make_identity(nc, ident[:])

        def load_x(s, a=0, b=T):
            nc.sync.dma_start(
                x_raw[s][:, :, a:b], xT[512 * s : 512 * (s + 1), a:b].rearrange("(p j) w -> p j w", j=4)
            )

        def load_w(m, e, s0=0, s1=PASSES):
            words = (w1_words, w3_words)[m]
            nc.sync.dma_start(
                w13[:, e, m, s0:s1].bitcast(I32), words[e, s0:s1].bitcast(I32).rearrange("s p c -> p s c")
            )

        def load_sc13(f):
            for m, scales in enumerate((w1_scales, w3_scales)):
                src = scales[2 * f : 2 * f + 2].bitcast(I32).rearrange("e s (q r) c -> r q (e s) c", r=4)
                dst = sc13[f][:].bitcast(I32)
                for r in range(4):
                    nc.sync.dma_start(dst[r:P:32, m, :, :], src[r])

        def load_sc2():
            src = w2_scales[:, 0].bitcast(I32).rearrange("e (q r) c -> r q e c", r=4)
            dst = sc2[:].bitcast(I32)
            for r in range(4):
                nc.sync.dma_start(dst[r:P:32, :, :], src[r])

        def load_w2():
            nc.sync.dma_start(w2_t[:].bitcast(I32), w2_words[:, 0].bitcast(I32).rearrange("e p c -> p e c"))

        nc.sync.dma_start(offsets[:], offs)
        load_x(0, 0, 256)
        load_x(0, 256, 512)
        load_x(1)
        load_sc13(0)
        load_x(2)
        load_w(0, 0, 0, 3)
        load_w(1, 0, 0, 3)
        load_w(0, 1, 0, 3)
        load_w(1, 1, 0, 3)
        load_sc13(1)
        load_sc2()
        load_w(0, 2, 0, 3)
        load_w(1, 2, 0, 3)
        load_w(0, 3, 0, 3)
        load_w(1, 3, 0, 3)
        load_w2()

        def interleave(s, a, v, b):
            dst = x_grp[s][:].rearrange("p (c i) t -> p c t i", i=4)
            src = x_raw[s][:].rearrange("p t (c i) -> p c t i", i=4)
            if v > a:
                nc.vector.tensor_copy(dst[:, a // 4 : v // 4], src[:, a // 4 : v // 4])
            if b > v:
                nc.scalar.activation(dst[:, v // 4 : b // 4], src[:, v // 4 : b // 4], COPY)

        def quantize(s, a, b):
            nc.vector.quantize_mx(
                out=x_words[s][:, a:b].bitcast(E4M3),
                scales=x_bytes[s][:, a:b],
                in_=x_grp[s][:, a:b].rearrange("p c t -> p (c t)"),
            )

        def gather(s, a, b):
            lst = offsets[:, a // 16 : b // 16]
            nc.vector.tensor_copy(g_words[s][:, a:b], x_words[s][:].indirect(lst))
            nc.vector.tensor_copy(g_bytes[s][:, a:b], x_bytes[s][:].indirect(lst))

        def product(e, m, name):
            acc = psum.tile([P, H], F32, name=name)
            cols = slice(C * e, C * (e + 1))
            for s in range(PASSES):
                nc.tensor.matmul_mx(
                    out=acc[:],
                    lhsT=g_words[s][:, cols].bitcast(E4M3),
                    lhsT_scale=g_bytes[s][:, cols],
                    rhs=w13[:, e, m, s, :].bitcast(E2M1),
                    rhs_scale=sc13[e // 2][:, m, PASSES * (e % 2) + s, :],
                    start=(s == 0),
                    stop=(s == PASSES - 1),
                )
            return acc

        def first_layer(e):
            acc_a = product(e, 0, "acc_a")
            act = work.tile([P, H], F32, name="act")
            nc.scalar.activation(act[:], acc_a[:], RELU)
            acc_b = product(e, 1, "acc_b")
            h = work.tile([P, H], BF16, name="h")
            nc.vector.tensor_tensor(h[:], acc_b[:], act[:], MULT)
            return h

        def second_layer(e, h):
            turned = psum1.tile([P, 2, C], F32, name="turned")
            words = h[:].bitcast(F32)
            for u in range(2):
                nc.tensor.transpose(turned[:, u, :], words[:, u::2], ident[:])
            h_grp = work.tile([P, C, 4], BF16, name="h_grp", align_bytes=64)
            h_flat = h_grp[:].rearrange("p c t -> p (c t)")
            nc.scalar.copy(h_flat.bitcast(F32).rearrange("p (c u) -> p c u", u=2), turned[:].rearrange("p u c -> p c u"))
            h_words = work.tile([P, C], U32, name="h_words", align_bytes=64)
            h_bytes = work.tile([P, C], U8, name="h_bytes", align_bytes=64)
            nc.vector.quantize_mx(out=h_words[:].bitcast(E4M3), scales=h_bytes[:], in_=h_flat)
            y = psum1.tile([P, 2, C], F32, name="y")
            for half in range(2):
                nc.tensor.matmul_mx(
                    out=y[:, half, :],
                    lhsT=w2_t[:, e, 2 * P * half : 2 * P * (half + 1)].bitcast(E2M1),
                    lhsT_scale=sc2[:, e, P * half : P * (half + 1)],
                    rhs=h_words[:].bitcast(E4M3),
                    rhs_scale=h_bytes[:],
                    start=True,
                    stop=True,
                )
            nc.scalar.copy(o_sb[:, :, :, e, :], y[:].rearrange("p h (m u) -> p h m u", m=R))

        for s, a, v, b in CHUNKS:
            interleave(s, a, v, b)
            quantize(s, a, b)
            if b == T:
                gather(s, 0, 256)
                gather(s, 256, 512)
        for e in range(E):
            second_layer(e, first_layer(e))
        for half, queue in enumerate((nc.sync, nc.scalar)):
            queue.dma_start(out[P * half : P * (half + 1), :], o_sb[:, half].rearrange("p m e u -> p (m e u)"))
